import numpy as np
import ml_dtypes


def mxq(x, axis, fmt="e4m3"):
    dtype, down = {"e4m3": (ml_dtypes.float8_e4m3fn, 7), "e5m2": (ml_dtypes.float8_e5m2, 14)}[fmt]
    v = np.moveaxis(np.asarray(x, np.float32).astype(ml_dtypes.bfloat16).astype(np.float64), axis, -1)
    blocks = v.reshape(v.shape[:-1] + (-1, 32))
    amax = np.abs(blocks).max(-1, keepdims=True)
    byte = np.maximum(np.where(amax > 0, np.frexp(amax)[1] - 1 + 127, 0) - down, 1)
    scale = np.exp2(byte - 127.0)
    codes = (blocks / scale).astype(np.float32).astype(dtype).astype(np.float64)
    return np.moveaxis((codes * scale).reshape(v.shape), -1, axis)


WIDE = False


def mx_kscale(k):
    if not WIDE:
        return np.ones(k)
    levels = np.array([10, -10, 5, -5, 0])
    if k % 512:
        return np.exp2(np.random.permutation(np.resize(levels, k // 32))).repeat(32)
    a = np.empty((k // 512, 16))
    for p in range(k // 512):
        a[p, :8] = np.random.permutation(np.resize(levels, 8))
        for g in range(8):
            far = levels[np.abs(levels - a[p, g]) >= 10]
            a[p, g + 8] = far[np.random.randint(len(far))]
    return np.exp2(a.ravel()).repeat(32)


def f64(x):
    return np.asarray(x).astype(np.float64)


def striped(idx):
    return np.tile(np.asarray(idx).reshape(-1, 16).T, (8, 1)).astype(np.uint16)


def unstriped(offs):
    return offs[:16].T.reshape(-1).astype(np.int64)


def striped8(idx):
    return np.asarray(idx).reshape(8, -1, 16).transpose(0, 2, 1).reshape(128, -1).astype(np.uint16)


def unstriped8(offs):
    return offs.reshape(8, 16, -1).transpose(0, 2, 1).reshape(8, -1).astype(np.int64)


def pick8(x, idx, run):
    r = np.arange(len(x))
    return x[r[:, None], idx[r % (8 * run) // run]]


E2M1 = np.array([0.0, 0.5, 1.0, 1.5, 2.0, 3.0, 4.0, 6.0, -0.0, -0.5, -1.0, -1.5, -2.0, -3.0, -4.0, -6.0])


def pack_weight(w, fmt):
    k, n = w.shape
    w = f64(np.asarray(w, np.float32).astype(ml_dtypes.bfloat16)).reshape(k // 32, 32, n)
    amax = np.abs(w).max(1)
    if fmt == "e4m3":
        byte = np.frexp(amax)[1] - 1 + 127 - 7
    else:
        mant, ex = np.frexp(amax / 6.0)
        byte = np.where(mant > 0.5, ex, ex - 1) + 127
    byte = np.clip(np.where(amax > 0, byte, 1), 1, 254)
    scaled = (w * np.exp2(127.0 - byte)[:, None, :]).reshape(k, n).astype(np.float32)
    by_word = np.ascontiguousarray(scaled.reshape(k // 512, 128, 4, n).transpose(0, 1, 3, 2))
    if fmt == "e4m3":
        words = by_word.astype(ml_dtypes.float8_e4m3fn).view(np.uint8)
    else:
        c = by_word.astype(ml_dtypes.float4_e2m1fn).view(np.uint8) & 0xF
        words = (c[..., 0::2] | (c[..., 1::2] << 4)).reshape(k // 512, 128, 2 * n)
    return np.ascontiguousarray(words), np.ascontiguousarray(byte.astype(np.uint8).reshape(k // 512, 16, n))


def unpack_weight(words, scales, fmt):
    g, _, n = scales.shape
    words = np.ascontiguousarray(words).reshape(g, 128, n, -1)
    if fmt == "e4m3":
        vals = words.view(ml_dtypes.float8_e4m3fn).astype(np.float64)
    else:
        nib = np.empty((g, 128, n, 4), np.uint8)
        nib[..., 0::2] = words & 0xF
        nib[..., 1::2] = words >> 4
        vals = E2M1[nib]
    vals = vals * np.repeat(np.exp2(scales.astype(np.float64) - 127.0), 8, axis=1)[..., None]
    return vals.transpose(0, 1, 3, 2).reshape(g * 512, n)


K, J, R, T, C, N, U, E, G = 512, 384, 512, 2048, 512, 256, 1024, 256, 512


def setup_inputs():
    n = np.random.standard_normal
    idx = np.random.permutation(T)[:J]
    idx2 = np.stack([np.random.permutation(C)[:J] for _ in range(8)])
    idx3 = np.stack([np.random.permutation(C)[:J] for _ in range(8)])
    idx4 = np.stack([np.random.permutation(U)[:C] for _ in range(8)])
    idx5 = np.stack([np.random.permutation(U)[:E] for _ in range(8)])
    idx6 = np.stack([np.random.permutation(G)[:E] for _ in range(8)])
    fk = mx_kscale(K)
    fr = mx_kscale(R)
    xtp = pack_weight(n((K, T)) * fk[:, None], "e2m1")
    wp = pack_weight(n((K, R)) * 1 / np.sqrt(K) / fk[:, None] * fr, "e4m3")
    w2p = pack_weight(n((K, R)) * 1 / np.sqrt(K) / fk[:, None] * fr, "e4m3")
    wbp = pack_weight(n((R, N)) * 1 / np.sqrt(R) / fr[:, None], "e4m3")
    wop = pack_weight(n((R, N)) * 1 / np.sqrt(R) / fr[:, None], "e2m1")
    return {
        "xt_words": xtp[0],
        "xt_scales": xtp[1],
        "w_words": wp[0],
        "w_scales": wp[1],
        "w2_words": w2p[0],
        "w2_scales": w2p[1],
        "wb_words": wbp[0],
        "wb_scales": wbp[1],
        "wo_words": wop[0],
        "wo_scales": wop[1],
        "se": (np.random.uniform(0.5, 1.6, (N, 1))).astype(np.float32),
        "offs": striped(idx),
        "offs2": striped8(idx2),
        "offs3": striped8(idx3),
        "offs4": striped8(idx4),
        "offs5": striped8(idx5),
        "offs6": striped8(idx6),
    }


def reference(xt_words, xt_scales, w_words, w_scales, w2_words, w2_scales, wb_words, wb_scales, wo_words, wo_scales, se, offs, offs2, offs3, offs4, offs5, offs6):
    idx = unstriped(offs)
    idx2 = unstriped8(offs2)
    idx3 = unstriped8(offs3)
    idx4 = unstriped8(offs4)
    idx5 = unstriped8(offs5)
    idx6 = unstriped8(offs6)
    xtu = unpack_weight(xt_words, xt_scales, "e2m1")
    wu = unpack_weight(w_words, w_scales, "e4m3")
    w2u = unpack_weight(w2_words, w2_scales, "e4m3")
    wbu = unpack_weight(wb_words, wb_scales, "e4m3")
    wou = unpack_weight(wo_words, wo_scales, "e2m1")
    xtidxg = xtu[:, idx]
    a = wu.T @ xtidxg
    b = w2u.T @ xtidxg
    pw = np.zeros((R, C))
    pw[np.arange(R)[:, None], idx2[np.arange(R) % 512 // 64]] = a
    pv = np.zeros((R, C))
    pv[np.arange(R)[:, None], idx3[np.arange(R) % 512 // 64]] = b
    pwq = mxq(pw, 0, "e4m3")
    pvq = mxq(pv, 0, "e4m3")
    p = wbu.T @ pwq + wou.T @ pvq
    m0 = np.zeros((N, U))
    m0[np.arange(N)[:, None], idx4[np.arange(N) % 128 // 16]] = p
    m1 = pick8(m0, idx5, 16) * f64(se)
    y = np.zeros((N, G))
    y[np.arange(N)[:, None], idx6[np.arange(N) % 128 // 16]] = m1
    return y

@@ -1,0 +1,242 @@
+from contextlib import ExitStack
+
+import concourse.mybir as mybir
+
+F32 = mybir.dt.float32
+BF16 = mybir.dt.bfloat16
+I32 = mybir.dt.int32
+U16 = mybir.dt.uint16
+U8 = mybir.dt.uint8
+FP8X4 = mybir.dt.float8_e4m3fn_x4
+FP4X4 = mybir.dt.float4_e2m1fn_x4
+COPY = mybir.ActivationFunctionType.Copy
+
+P = 128
+PACK = 4
+K, J, R, T, C, N, U, E, G = 512, 384, 512, 2048, 512, 256, 1024, 256, 512
+FLOPS = 2 * (2 * K * R * J) + 2 * (2 * R * N * C)
+
+SLOT_RUNS = ((0, 256), (256, 384))
+PAGE_RUNS = ((0, 128), (128, 256), (256, 512))
+
+
+def tile_picked_tokens_plain_twin_twopages_pages_endrelay_kernel(
+    tc, xt_words, xt_scales, w_words, w_scales, w2_words, w2_scales, wb_words, wb_scales,
+    wo_words, wo_scales, se, offs, offs2, offs3, offs4, offs5, offs6, out,
+):
+    nc = tc.nc
+    with ExitStack() as ctx:
+        keep = ctx.enter_context(tc.tile_pool(name="keep", bufs=1))
+        pages = ctx.enter_context(tc.tile_pool(name="pages", bufs=3))
+        results = ctx.enter_context(tc.tile_pool(name="results", bufs=8))
+        psum_slots = ctx.enter_context(tc.psum_pool(name="psum_slots", bufs=4))
+        psum_pages = ctx.enter_context(tc.psum_pool(name="psum_pages", bufs=1))
+
+        def load_list(dram, name):
+            tile = keep.tile(list(dram.shape), U16, name=name)
+            nc.sync.dma_start(tile[:], dram)
+            return tile
+
+        def scale_tile(width, name):
+            tile = keep.tile([P, width], U8, name=name, tag=name, align_bytes=64)
+            nc.vector.memset(tile[:].bitcast(I32), 0)
+            return tile
+
+        def load_scale_rows(tile, dram):
+            for q in range(4):
+                nc.sync.dma_start(tile[32 * q:32 * q + 4, :].bitcast(I32), dram[0, 4 * q:4 * q + 4, :].bitcast(I32))
+
+        def stage_scale_rows(dram, name):
+            tile = keep.tile([4, 4, R // 4], I32, name=name, tag=name)
+            nc.sync.dma_start(tile[:], dram[0].bitcast(I32).rearrange("(q i) n -> i q n", i=4))
+            return tile
+
+        def spread_scale_rows(tile, staged):
+            for q in range(4):
+                nc.vector.tensor_copy(out=tile[32 * q:32 * q + 4, :].bitcast(I32), in_=staged[:, q, :])
+
+        def load_e4m3_words(dram, name, tag):
+            tile = keep.tile([P, dram.shape[2]], I32, name=name, tag=tag, align_bytes=64)
+            nc.sync.dma_start(tile[:], dram[0].rearrange("p n t -> p (n t)").bitcast(I32))
+            return tile
+
+        def deal(source, dtype, first, last, name):
+            tile = keep.tile([P, (last - first) * P], dtype, name=name, align_bytes=64)
+            nc.vector.tensor_copy(
+                out=tile[:].rearrange("p (t m) -> p m t", m=P),
+                in_=source[:].rearrange("p (m t) -> p m t", t=PACK)[:, :, first:last],
+            )
+            return tile
+
+        def zeroed(pool, width, name, tag):
+            tile = pool.tile([P, width], F32, name=name, tag=tag, align_bytes=64)
+            nc.vector.memset(tile[:], 0.0)
+            return tile
+
+        xt_scale_table = scale_tile(T, "xt_scale_table")
+        w_scale_rows = scale_tile(R, "w_scale_rows")
+        w_staged = stage_scale_rows(w_scales, "w_staged")
+        xt_word_table = keep.tile([P, T], U16, name="xt_word_table", tag="xt_word_table", align_bytes=64)
+        nc.sync.dma_start(xt_word_table[:].bitcast(I32), xt_words[0].bitcast(I32))
+        token_list = load_list(offs, "token_list")
+        load_scale_rows(xt_scale_table, xt_scales)
+        w_loaded = load_e4m3_words(w_words, "w_loaded", "w_loaded")
+        first_page_lists = load_list(offs2, "first_page_lists")
+        spread_scale_rows(w_scale_rows, w_staged)
+
+        x_words = keep.tile([P, J], U16, name="x_words", align_bytes=64)
+        x_scales = keep.tile([P, J], U8, name="x_scales", align_bytes=64)
+        nc.vector.tensor_copy(out=x_words[:], in_=xt_word_table[:].indirect(token_list[:]))
+        nc.vector.tensor_copy(out=x_scales[:], in_=xt_scale_table[:].indirect(token_list[:]))
+
+        def dealt_matrix(words, scales, name):
+            parts = []
+            for first, last in ((0, 1), (1, PACK)):
+                part_words = deal(words, I32, first, last, f"{name}_words{first}")
+                part_scales = deal(scales, U8, first, last, f"{name}_scales{first}")
+                for t in range(last - first):
+                    cols = slice(t * P, (t + 1) * P)
+                    parts.append((part_words[:, cols], part_scales[:, cols]))
+            return parts
+
+        def slot_results(matrix, t, on_scalar):
+            words, scales = matrix[t]
+            acc = psum_slots.tile([P, J], F32, name="acc")
+            for lo, hi in SLOT_RUNS:
+                nc.tensor.matmul_mx(
+                    acc[:, lo:hi], lhsT=words.bitcast(FP8X4), lhsT_scale=scales,
+                    rhs=x_words[:, lo:hi].bitcast(FP4X4), rhs_scale=x_scales[:, lo:hi], start=True, stop=True,
+                )
+            result = results.tile([P, J], F32, name="result")
+            if on_scalar:
+                nc.scalar.activation(out=result[:], in_=acc[:], func=COPY)
+            else:
+                nc.vector.tensor_copy(out=result[:], in_=acc[:])
+            return result
+
+        def scatter_on_page(result, lists, name):
+            page = zeroed(pages, C, name, "page")
+            nc.scalar.activation(out=page[:].indirect(lists[:]), in_=result[:], func=COPY)
+            return page
+
+        def quantise(grouped, width, name):
+            codes = keep.tile([P, width], I32, name=f"{name}_codes", align_bytes=64)
+            scales = keep.tile([P, width], U8, name=f"{name}_scales", align_bytes=64)
+            nc.vector.quantize_mx(out=codes[:].bitcast(FP8X4), scales=scales[:], in_=grouped[:].rearrange("p c t -> p (c t)"))
+            return codes, scales
+
+        w_dealt = dealt_matrix(w_loaded, w_scale_rows, "w")
+
+        w2_scale_rows = scale_tile(R, "w2_scale_rows")
+        wb_scale_rows = scale_tile(N, "wb_scale_rows")
+        wo_scale_rows = scale_tile(N, "wo_scale_rows")
+        w2_loaded = load_e4m3_words(w2_words, "w2_loaded", "w2_loaded")
+        w2_staged = stage_scale_rows(w2_scales, "w2_staged")
+        second_page_lists = load_list(offs3, "second_page_lists")
+        wb_loaded = load_e4m3_words(wb_words, "wb_loaded", "wb_loaded")
+        load_scale_rows(wb_scale_rows, wb_scales)
+        wo_loaded = keep.tile([P, 2 * N], U8, name="wo_loaded", align_bytes=64)
+        nc.sync.dma_start(wo_loaded[:].bitcast(I32), wo_words[0].bitcast(I32))
+        load_scale_rows(wo_scale_rows, wo_scales)
+        relay_put_lists = load_list(offs4, "relay_put_lists")
+        relay_get_lists = load_list(offs5, "relay_get_lists")
+        last_page_lists = load_list(offs6, "last_page_lists")
+        relay_weights = []
+        for n in range(N // P):
+            weight = keep.tile([P, 1], F32, name=f"relay_weight{n}")
+            nc.sync.dma_start(weight[:], se[n * P:(n + 1) * P, :])
+            relay_weights.append(weight)
+
+        first_grouped = keep.tile([P, C, PACK], BF16, name="first_grouped", align_bytes=64)
+        second_grouped = [
+            keep.tile([P, hi - lo, PACK], BF16, name=f"second_grouped{lo}", align_bytes=64) for lo, hi in PAGE_RUNS
+        ]
+        first_results = [slot_results(w_dealt, t, on_scalar=(t == 0)) for t in range(PACK)]
+        first_pages = [scatter_on_page(first_results[t], first_page_lists, f"first_page{t}") for t in range(PACK - 1)]
+        spread_scale_rows(w2_scale_rows, w2_staged)
+        w2_dealt = dealt_matrix(w2_loaded, w2_scale_rows, "w2")
+
+        second_results = []
+        second_pages = []
+        for t in range(PACK):
+            nc.vector.tensor_copy(out=first_grouped[:, :, t], in_=first_pages[t][:])
+            if t == 0:
+                first_pages.append(scatter_on_page(first_results[PACK - 1], first_page_lists, "first_page3"))
+            else:
+                second_pages.append(scatter_on_page(second_results[t - 1], second_page_lists, f"second_page{t - 1}"))
+            second_results.append(slot_results(w2_dealt, t, on_scalar=False))
+        first_codes, first_scales = quantise(first_grouped, C, "first")
+        relay_pages = [zeroed(keep, U, f"relay_page{n}", tag) for n, tag in enumerate(("w_loaded", "w2_loaded"))]
+
+        def round_second(t, run):
+            lo, hi = PAGE_RUNS[run]
+            nc.vector.tensor_copy(out=second_grouped[run][:, :, t], in_=second_pages[t][:, lo:hi])
+
+        banks = {}
+        for run, (lo, hi) in enumerate(PAGE_RUNS):
+            if run == 0:
+                for n in range(N // P):
+                    single = psum_pages.tile([P, hi - lo], F32, name=f"page_sum{run}_{n}")
+                    banks[run, n] = single[:]
+            else:
+                both = psum_pages.tile([P, N // P, hi - lo], F32, name=f"page_sum{run}")
+                banks[run] = both
+                for n in range(N // P):
+                    banks[run, n] = both[:, n, :]
+            for n in range(N // P):
+                rows = slice(n * P, (n + 1) * P)
+                nc.tensor.matmul_mx(
+                    banks[run, n], lhsT=wb_loaded[:, rows].bitcast(FP8X4), lhsT_scale=wb_scale_rows[:, rows],
+                    rhs=first_codes[:, lo:hi].bitcast(FP8X4), rhs_scale=first_scales[:, lo:hi],
+                    start=(run == 0 or n == 0), stop=False,
+                )
+
+        last_pages = []
+        for t in range(PACK - 1):
+            for run in range(len(PAGE_RUNS)):
+                round_second(t, run)
+            if t == 0:
+                second_pages.append(scatter_on_page(second_results[PACK - 1], second_page_lists, "second_page3"))
+            else:
+                last_pages.append(zeroed(pages, G, f"last_page{t - 1}", "page"))
+
+        def finish_run(run):
+            lo, hi = PAGE_RUNS[run]
+            codes, scales = quantise(second_grouped[run], hi - lo, f"second{run}")
+            for n in range(N // P):
+                nc.tensor.matmul_mx(
+                    banks[run, n], lhsT=wo_loaded[:, 2 * n * P:2 * (n + 1) * P].bitcast(FP4X4),
+                    lhsT_scale=wo_scale_rows[:, n * P:(n + 1) * P],
+                    rhs=codes[:].bitcast(FP8X4), rhs_scale=scales[:],
+                    start=False, stop=(run == 0 or n == N // P - 1),
+                )
+
+        round_second(PACK - 1, 0)
+        round_second(PACK - 1, 1)
+        finish_run(0)
+        round_second(PACK - 1, 2)
+        finish_run(1)
+        finish_run(2)
+
+        for run, (lo, hi) in enumerate(PAGE_RUNS):
+            sums = keep.tile([P, N // P, hi - lo], F32, name=f"sums{run}")
+            if run == 0:
+                for n in range(N // P):
+                    nc.scalar.copy(out=sums[:, n, :], in_=banks[run, n])
+            else:
+                nc.vector.tensor_copy(out=sums[:], in_=banks[run][:])
+            for n in range(N // P):
+                nc.scalar.activation(
+                    out=relay_pages[n][:].indirect(relay_put_lists[:, lo // 16:hi // 16]), in_=sums[:, n, :], func=COPY
+                )
+
+        relayed = []
+        for n in range(N // P):
+            values = keep.tile([P, E], F32, name=f"relayed{n}")
+            nc.scalar.activation(
+                out=values[:], in_=relay_pages[n][:].indirect(relay_get_lists[:]), func=COPY, scale=relay_weights[n][:]
+            )
+            relayed.append(values)
+        for n in range(N // P):
+            nc.scalar.activation(out=last_pages[n][:].indirect(last_page_lists[:]), in_=relayed[n][:], func=COPY)
+            nc.sync.dma_start(out[n * P:(n + 1) * P, :], last_pages[n][:])

@@ -16,7 +16,15 @@ PACK = 4
 K, J, R, T, C, N, U, E, G = 512, 384, 512, 2048, 512, 256, 1024, 256, 512
 FLOPS = 2 * (2 * K * R * J) + 2 * (2 * R * N * C)
 
-SLOT_RUNS = ((0, 256), (256, 384))
+AT_W = 0
+AT_HEAD = 2048
+AT_PAGES = 4096
+AT_XT_WORDS = 8192
+AT_XT_SCALES = 12288
+AT_W_SCALES = 14336
+AT_W2 = 14848
+GATHER = 256
+EARLY = 2
 PAGE_RUNS = ((0, 128), (128, 256), (256, 512))
 
 
@@ -27,8 +35,8 @@ def tile_picked_tokens_plain_twin_twopages_pages_endrelay_kernel(
     nc = tc.nc
     with ExitStack() as ctx:
         keep = ctx.enter_context(tc.tile_pool(name="keep", bufs=1))
-        pages = ctx.enter_context(tc.tile_pool(name="pages", bufs=3))
-        results = ctx.enter_context(tc.tile_pool(name="results", bufs=8))
+        results = ctx.enter_context(tc.tile_pool(name="results", bufs=10))
+        shared = ctx.enter_context(tc.tile_pool(name="shared", bufs=1))
         psum_slots = ctx.enter_context(tc.psum_pool(name="psum_slots", bufs=4))
         psum_pages = ctx.enter_context(tc.psum_pool(name="psum_pages", bufs=1))
 
@@ -37,8 +45,8 @@ def tile_picked_tokens_plain_twin_twopages_pages_endrelay_kernel(
             nc.sync.dma_start(tile[:], dram)
             return tile
 
-        def scale_tile(width, name):
-            tile = keep.tile([P, width], U8, name=name, tag=name, align_bytes=64)
+        def scale_tile(width, name, offset):
+            tile = shared.tile([P, width], U8, name=name, align_bytes=64, offset=offset)
             nc.vector.memset(tile[:].bitcast(I32), 0)
             return tile
 
@@ -55,10 +63,8 @@ def tile_picked_tokens_plain_twin_twopages_pages_endrelay_kernel(
             for q in range(4):
                 nc.vector.tensor_copy(out=tile[32 * q:32 * q + 4, :].bitcast(I32), in_=staged[:, q, :])
 
-        def load_e4m3_words(dram, name, tag):
-            tile = keep.tile([P, dram.shape[2]], I32, name=name, tag=tag, align_bytes=64)
+        def load_e4m3_words(tile, dram):
             nc.sync.dma_start(tile[:], dram[0].rearrange("p n t -> p (n t)").bitcast(I32))
-            return tile
 
         def deal(source, dtype, first, last, name):
             tile = keep.tile([P, (last - first) * P], dtype, name=name, align_bytes=64)
@@ -68,30 +74,34 @@ def tile_picked_tokens_plain_twin_twopages_pages_endrelay_kernel(
             )
             return tile
 
-        def zeroed(pool, width, name, tag):
-            tile = pool.tile([P, width], F32, name=name, tag=tag, align_bytes=64)
+        def zeroed(width, name, offset):
+            tile = shared.tile([P, width], F32, name=name, align_bytes=64, offset=offset)
             nc.vector.memset(tile[:], 0.0)
             return tile
 
-        xt_scale_table = scale_tile(T, "xt_scale_table")
-        w_scale_rows = scale_tile(R, "w_scale_rows")
+        xt_scale_table = scale_tile(T, "xt_scale_table", AT_XT_SCALES)
+        w_scale_rows = scale_tile(R, "w_scale_rows", AT_W_SCALES)
         w_staged = stage_scale_rows(w_scales, "w_staged")
-        xt_word_table = keep.tile([P, T], U16, name="xt_word_table", tag="xt_word_table", align_bytes=64)
+        xt_word_table = shared.tile([P, T], U16, name="xt_word_table", align_bytes=64, offset=AT_XT_WORDS)
         nc.sync.dma_start(xt_word_table[:].bitcast(I32), xt_words[0].bitcast(I32))
         token_list = load_list(offs, "token_list")
         load_scale_rows(xt_scale_table, xt_scales)
-        w_loaded = load_e4m3_words(w_words, "w_loaded", "w_loaded")
+        w_loaded = shared.tile([P, R], I32, name="w_loaded", align_bytes=64, offset=AT_W)
+        load_e4m3_words(w_loaded, w_words)
         first_page_lists = load_list(offs2, "first_page_lists")
         spread_scale_rows(w_scale_rows, w_staged)
 
-        x_words = keep.tile([P, J], U16, name="x_words", align_bytes=64)
-        x_scales = keep.tile([P, J], U8, name="x_scales", align_bytes=64)
-        nc.vector.tensor_copy(out=x_words[:], in_=xt_word_table[:].indirect(token_list[:]))
-        nc.vector.tensor_copy(out=x_scales[:], in_=xt_scale_table[:].indirect(token_list[:]))
+        def gather_tokens(lo, offset, name):
+            entries = token_list[:, lo // 16:(lo + GATHER) // 16]
+            words = shared.tile([P, GATHER], U16, name=f"{name}_words", align_bytes=64, offset=offset)
+            scales = shared.tile([P, GATHER], U8, name=f"{name}_scales", align_bytes=64, offset=offset + 2 * GATHER)
+            nc.vector.tensor_copy(out=words[:], in_=xt_word_table[:].indirect(entries))
+            nc.vector.tensor_copy(out=scales[:], in_=xt_scale_table[:].indirect(entries))
+            return words, scales
 
-        def dealt_matrix(words, scales, name):
+        def dealt_matrix(words, scales, groups, name):
             parts = []
-            for first, last in ((0, 1), (1, PACK)):
+            for first, last in groups:
                 part_words = deal(words, I32, first, last, f"{name}_words{first}")
                 part_scales = deal(scales, U8, first, last, f"{name}_scales{first}")
                 for t in range(last - first):
@@ -99,24 +109,32 @@ def tile_picked_tokens_plain_twin_twopages_pages_endrelay_kernel(
                     parts.append((part_words[:, cols], part_scales[:, cols]))
             return parts
 
-        def slot_results(matrix, t, on_scalar):
-            words, scales = matrix[t]
-            acc = psum_slots.tile([P, J], F32, name="acc")
-            for lo, hi in SLOT_RUNS:
-                nc.tensor.matmul_mx(
-                    acc[:, lo:hi], lhsT=words.bitcast(FP8X4), lhsT_scale=scales,
-                    rhs=x_words[:, lo:hi].bitcast(FP4X4), rhs_scale=x_scales[:, lo:hi], start=True, stop=True,
-                )
-            result = results.tile([P, J], F32, name="result")
+        def product(acc, matrix_part, tokens, lo, hi):
+            nc.tensor.matmul_mx(
+                acc, lhsT=matrix_part[0].bitcast(FP8X4), lhsT_scale=matrix_part[1],
+                rhs=tokens[0][:, lo:hi].bitcast(FP4X4), rhs_scale=tokens[1][:, lo:hi], start=True, stop=True,
+            )
+
+        def slot_results(matrix_part, pieces, on_scalar=False):
+            width = sum(hi - lo for tokens, lo, hi in pieces)
+            acc = psum_slots.tile([P, width], F32, name="acc")
+            at = 0
+            for tokens, lo, hi in pieces:
+                product(acc[:, at:at + hi - lo], matrix_part, tokens, lo, hi)
+                at = at + hi - lo
+            result = results.tile([P, width], F32, name="result")
             if on_scalar:
                 nc.scalar.activation(out=result[:], in_=acc[:], func=COPY)
             else:
                 nc.vector.tensor_copy(out=result[:], in_=acc[:])
             return result
 
-        def scatter_on_page(result, lists, name):
-            page = zeroed(pages, C, name, "page")
-            nc.scalar.activation(out=page[:].indirect(lists[:]), in_=result[:], func=COPY)
+        def scatter(page, entries, values):
+            nc.scalar.activation(out=page[:].indirect(entries), in_=values, func=COPY)
+
+        def scatter_on_page(result, lists, t, name):
+            page = zeroed(C, f"{name}{t}", AT_PAGES + 4 * C * t)
+            scatter(page, lists[:], result[:])
             return page
 
         def quantise(grouped, width, name):
@@ -125,15 +143,27 @@ def tile_picked_tokens_plain_twin_twopages_pages_endrelay_kernel(
             nc.vector.quantize_mx(out=codes[:].bitcast(FP8X4), scales=scales[:], in_=grouped[:].rearrange("p c t -> p (c t)"))
             return codes, scales
 
-        w_dealt = dealt_matrix(w_loaded, w_scale_rows, "w")
+        head_tokens = gather_tokens(0, AT_HEAD, "head")
+        w_dealt = dealt_matrix(w_loaded, w_scale_rows, ((0, PACK),), "w")
+        first_pages = [zeroed(C, f"first_page{t}", AT_PAGES + 4 * C * t) for t in range(EARLY)]
+        early = [slot_results(w_dealt[t], ((head_tokens, 0, GATHER),), on_scalar=True) for t in range(EARLY)]
+        for t in range(EARLY):
+            scatter(first_pages[t], first_page_lists[:, :GATHER // 16], early[t][:])
+        tail_tokens = gather_tokens(J - GATHER, AT_W, "tail")
+        for t in range(EARLY):
+            result = slot_results(w_dealt[t], ((tail_tokens, 2 * GATHER - J, GATHER),))
+            scatter(first_pages[t], first_page_lists[:, GATHER // 16:], result[:])
+        all_slots = ((head_tokens, 0, J - GATHER), (tail_tokens, 0, GATHER))
 
-        w2_scale_rows = scale_tile(R, "w2_scale_rows")
-        wb_scale_rows = scale_tile(N, "wb_scale_rows")
-        wo_scale_rows = scale_tile(N, "wo_scale_rows")
-        w2_loaded = load_e4m3_words(w2_words, "w2_loaded", "w2_loaded")
+        w2_scale_rows = scale_tile(R, "w2_scale_rows", AT_W_SCALES)
+        wb_scale_rows = scale_tile(N, "wb_scale_rows", AT_XT_SCALES)
+        wo_scale_rows = scale_tile(N, "wo_scale_rows", AT_XT_SCALES + N)
+        w2_loaded = shared.tile([P, R], I32, name="w2_loaded", align_bytes=64, offset=AT_W2)
+        load_e4m3_words(w2_loaded, w2_words)
         w2_staged = stage_scale_rows(w2_scales, "w2_staged")
         second_page_lists = load_list(offs3, "second_page_lists")
-        wb_loaded = load_e4m3_words(wb_words, "wb_loaded", "wb_loaded")
+        wb_loaded = keep.tile([P, N], I32, name="wb_loaded", align_bytes=64)
+        load_e4m3_words(wb_loaded, wb_words)
         load_scale_rows(wb_scale_rows, wb_scales)
         wo_loaded = keep.tile([P, 2 * N], U8, name="wo_loaded", align_bytes=64)
         nc.sync.dma_start(wo_loaded[:].bitcast(I32), wo_words[0].bitcast(I32))
@@ -147,26 +177,23 @@ def tile_picked_tokens_plain_twin_twopages_pages_endrelay_kernel(
             nc.sync.dma_start(weight[:], se[n * P:(n + 1) * P, :])
             relay_weights.append(weight)
 
-        first_grouped = keep.tile([P, C, PACK], BF16, name="first_grouped", align_bytes=64)
-        second_grouped = [
-            keep.tile([P, hi - lo, PACK], BF16, name=f"second_grouped{lo}", align_bytes=64) for lo, hi in PAGE_RUNS
-        ]
-        first_results = [slot_results(w_dealt, t, on_scalar=(t == 0)) for t in range(PACK)]
-        first_pages = [scatter_on_page(first_results[t], first_page_lists, f"first_page{t}") for t in range(PACK - 1)]
+        for t in range(EARLY, PACK):
+            first_pages.append(scatter_on_page(slot_results(w_dealt[t], all_slots), first_page_lists, t, "first_page"))
         spread_scale_rows(w2_scale_rows, w2_staged)
-        w2_dealt = dealt_matrix(w2_loaded, w2_scale_rows, "w2")
+        w2_dealt = dealt_matrix(w2_loaded, w2_scale_rows, ((0, PACK),), "w2")
+        second_results = [slot_results(w2_dealt[t], all_slots) for t in range(PACK)]
 
-        second_results = []
+        first_grouped = shared.tile([P, C, PACK], BF16, name="first_grouped", align_bytes=64, offset=AT_W2)
         second_pages = []
         for t in range(PACK):
             nc.vector.tensor_copy(out=first_grouped[:, :, t], in_=first_pages[t][:])
-            if t == 0:
-                first_pages.append(scatter_on_page(first_results[PACK - 1], first_page_lists, "first_page3"))
-            else:
-                second_pages.append(scatter_on_page(second_results[t - 1], second_page_lists, f"second_page{t - 1}"))
-            second_results.append(slot_results(w2_dealt, t, on_scalar=False))
+            second_pages.append(scatter_on_page(second_results[t], second_page_lists, t, "second_page"))
         first_codes, first_scales = quantise(first_grouped, C, "first")
-        relay_pages = [zeroed(keep, U, f"relay_page{n}", tag) for n, tag in enumerate(("w_loaded", "w2_loaded"))]
+        relay_pages = [zeroed(U, f"relay_page{n}", offset) for n, offset in enumerate((AT_W, AT_W2))]
+        second_grouped = {}
+        for run in range(2):
+            lo, hi = PAGE_RUNS[run]
+            second_grouped[run] = keep.tile([P, hi - lo, PACK], BF16, name=f"second_grouped{run}", tag=f"second_grouped{run}", align_bytes=64)
 
         def round_second(t, run):
             lo, hi = PAGE_RUNS[run]
@@ -191,14 +218,9 @@ def tile_picked_tokens_plain_twin_twopages_pages_endrelay_kernel(
                     start=(run == 0 or n == 0), stop=False,
                 )
 
-        last_pages = []
         for t in range(PACK - 1):
-            for run in range(len(PAGE_RUNS)):
+            for run in range(2):
                 round_second(t, run)
-            if t == 0:
-                second_pages.append(scatter_on_page(second_results[PACK - 1], second_page_lists, "second_page3"))
-            else:
-                last_pages.append(zeroed(pages, G, f"last_page{t - 1}", "page"))
 
         def finish_run(run):
             lo, hi = PAGE_RUNS[run]
@@ -211,14 +233,8 @@ def tile_picked_tokens_plain_twin_twopages_pages_endrelay_kernel(
                     start=False, stop=(run == 0 or n == N // P - 1),
                 )
 
-        round_second(PACK - 1, 0)
-        round_second(PACK - 1, 1)
-        finish_run(0)
-        round_second(PACK - 1, 2)
-        finish_run(1)
-        finish_run(2)
-
-        for run, (lo, hi) in enumerate(PAGE_RUNS):
+        def relay_run(run):
+            lo, hi = PAGE_RUNS[run]
             sums = keep.tile([P, N // P, hi - lo], F32, name=f"sums{run}")
             if run == 0:
                 for n in range(N // P):
@@ -226,9 +242,21 @@ def tile_picked_tokens_plain_twin_twopages_pages_endrelay_kernel(
             else:
                 nc.vector.tensor_copy(out=sums[:], in_=banks[run][:])
             for n in range(N // P):
-                nc.scalar.activation(
-                    out=relay_pages[n][:].indirect(relay_put_lists[:, lo // 16:hi // 16]), in_=sums[:, n, :], func=COPY
-                )
+                scatter(relay_pages[n], relay_put_lists[:, lo // 16:hi // 16], sums[:, n, :])
+
+        round_second(PACK - 1, 0)
+        round_second(PACK - 1, 1)
+        finish_run(0)
+        finish_run(1)
+        relay_run(0)
+        relay_run(1)
+        lo, hi = PAGE_RUNS[2]
+        second_grouped[2] = keep.tile([P, hi - lo, PACK], BF16, name="second_grouped2", tag="second_grouped0", align_bytes=64)
+        for t in range(PACK):
+            round_second(t, 2)
+        finish_run(2)
+        relay_run(2)
+        last_pages = [zeroed(G, f"last_page{n}", AT_PAGES + 4 * C * n) for n in range(N // P)]
 
         relayed = []
         for n in range(N // P):

@@ -25,7 +25,7 @@ AT_W_SCALES = 14336
 AT_W2 = 14848
 GATHER = 256
 EARLY = 2
-PAGE_RUNS = ((0, 128), (128, 256), (256, 512))
+PAGE_RUNS = ((0, 128), (128, 384), (384, 512))
 
 
 def tile_picked_tokens_plain_twin_twopages_pages_endrelay_kernel(
@@ -68,9 +68,10 @@ def tile_picked_tokens_plain_twin_twopages_pages_endrelay_kernel(
 
         def deal(source, dtype, first, last, name):
             tile = keep.tile([P, (last - first) * P], dtype, name=name, align_bytes=64)
+            order = "p m t" if dtype == I32 else "p t m"
             nc.vector.tensor_copy(
-                out=tile[:].rearrange("p (t m) -> p m t", m=P),
-                in_=source[:].rearrange("p (m t) -> p m t", t=PACK)[:, :, first:last],
+                out=tile[:].rearrange(f"p (t m) -> {order}", m=P),
+                in_=source[:].rearrange(f"p (m t) -> {order}", t=PACK),
             )
             return tile
 

@@ -50,9 +50,9 @@ def tile_picked_tokens_plain_twin_twopages_pages_endrelay_kernel(
             nc.vector.memset(tile[:].bitcast(I32), 0)
             return tile
 
-        def load_scale_rows(tile, dram):
+        def load_scale_rows(tile, dram, queue=nc.sync):
             for q in range(4):
-                nc.sync.dma_start(tile[32 * q:32 * q + 4, :].bitcast(I32), dram[0, 4 * q:4 * q + 4, :].bitcast(I32))
+                queue.dma_start(tile[32 * q:32 * q + 4, :].bitcast(I32), dram[0, 4 * q:4 * q + 4, :].bitcast(I32))
 
         def stage_scale_rows(dram, name):
             tile = keep.tile([4, 4, R // 4], I32, name=name, tag=name)
@@ -86,7 +86,7 @@ def tile_picked_tokens_plain_twin_twopages_pages_endrelay_kernel(
         xt_word_table = shared.tile([P, T], U16, name="xt_word_table", align_bytes=64, offset=AT_XT_WORDS)
         nc.sync.dma_start(xt_word_table[:].bitcast(I32), xt_words[0].bitcast(I32))
         token_list = load_list(offs, "token_list")
-        load_scale_rows(xt_scale_table, xt_scales)
+        load_scale_rows(xt_scale_table, xt_scales, nc.scalar)
         w_loaded = shared.tile([P, R], I32, name="w_loaded", align_bytes=64, offset=AT_W)
         load_e4m3_words(w_loaded, w_words)
         first_page_lists = load_list(offs2, "first_page_lists")

from contextlib import ExitStack

import concourse.mybir as mybir

F32 = mybir.dt.float32
BF16 = mybir.dt.bfloat16
I32 = mybir.dt.int32
U16 = mybir.dt.uint16
U8 = mybir.dt.uint8
FP8X4 = mybir.dt.float8_e4m3fn_x4
FP4X4 = mybir.dt.float4_e2m1fn_x4
COPY = mybir.ActivationFunctionType.Copy

P = 128
PACK = 4
K, J, R, T, C, N, U, E, G = 512, 384, 512, 2048, 512, 256, 1024, 256, 512
FLOPS = 2 * (2 * K * R * J) + 2 * (2 * R * N * C)

AT_W = 0
AT_HEAD = 2048
AT_PAGES = 4096
AT_XT_WORDS = 8192
AT_XT_SCALES = 12288
AT_W_SCALES = 14336
AT_W2 = 14848
GATHER = 256
EARLY = 2
PAGE_RUNS = ((0, 128), (128, 384), (384, 512))


def tile_picked_tokens_plain_twin_twopages_pages_endrelay_kernel(
    tc, xt_words, xt_scales, w_words, w_scales, w2_words, w2_scales, wb_words, wb_scales,
    wo_words, wo_scales, se, offs, offs2, offs3, offs4, offs5, offs6, out,
):
    nc = tc.nc
    with ExitStack() as ctx:
        keep = ctx.enter_context(tc.tile_pool(name="keep", bufs=1))
        results = ctx.enter_context(tc.tile_pool(name="results", bufs=10))
        shared = ctx.enter_context(tc.tile_pool(name="shared", bufs=1))
        psum_slots = ctx.enter_context(tc.psum_pool(name="psum_slots", bufs=4))
        psum_pages = ctx.enter_context(tc.psum_pool(name="psum_pages", bufs=1))

        def load_list(dram, name):
            tile = keep.tile(list(dram.shape), U16, name=name)
            nc.sync.dma_start(tile[:], dram)
            return tile

        def scale_tile(width, name, offset):
            tile = shared.tile([P, width], U8, name=name, align_bytes=64, offset=offset)
            nc.vector.memset(tile[:].bitcast(I32), 0)
            return tile

        def load_scale_rows(tile, dram, queue=nc.sync):
            for q in range(4):
                queue.dma_start(tile[32 * q:32 * q + 4, :].bitcast(I32), dram[0, 4 * q:4 * q + 4, :].bitcast(I32))

        def stage_scale_rows(dram, name):
            tile = keep.tile([4, 4, R // 4], I32, name=name, tag=name)
            nc.sync.dma_start(tile[:], dram[0].bitcast(I32).rearrange("(q i) n -> i q n", i=4))
            return tile

        def spread_scale_rows(tile, staged):
            for q in range(4):
                nc.vector.tensor_copy(out=tile[32 * q:32 * q + 4, :].bitcast(I32), in_=staged[:, q, :])

        def load_e4m3_words(tile, dram):
            nc.sync.dma_start(tile[:], dram[0].rearrange("p n t -> p (n t)").bitcast(I32))

        def deal(source, dtype, first, last, name):
            tile = keep.tile([P, (last - first) * P], dtype, name=name, align_bytes=64)
            order = "p m t" if dtype == I32 else "p t m"
            nc.vector.tensor_copy(
                out=tile[:].rearrange(f"p (t m) -> {order}", m=P),
                in_=source[:].rearrange(f"p (m t) -> {order}", t=PACK),
            )
            return tile

        def zeroed(width, name, offset):
            tile = shared.tile([P, width], F32, name=name, align_bytes=64, offset=offset)
            nc.vector.memset(tile[:], 0.0)
            return tile

        xt_scale_table = scale_tile(T, "xt_scale_table", AT_XT_SCALES)
        w_scale_rows = scale_tile(R, "w_scale_rows", AT_W_SCALES)
        w_staged = stage_scale_rows(w_scales, "w_staged")
        xt_word_table = shared.tile([P, T], U16, name="xt_word_table", align_bytes=64, offset=AT_XT_WORDS)
        nc.sync.dma_start(xt_word_table[:].bitcast(I32), xt_words[0].bitcast(I32))
        token_list = load_list(offs, "token_list")
        load_scale_rows(xt_scale_table, xt_scales, nc.scalar)
        w_loaded = shared.tile([P, R], I32, name="w_loaded", align_bytes=64, offset=AT_W)
        load_e4m3_words(w_loaded, w_words)
        first_page_lists = load_list(offs2, "first_page_lists")
        spread_scale_rows(w_scale_rows, w_staged)

        def gather_tokens(lo, offset, name):
            entries = token_list[:, lo // 16:(lo + GATHER) // 16]
            words = shared.tile([P, GATHER], U16, name=f"{name}_words", align_bytes=64, offset=offset)
            scales = shared.tile([P, GATHER], U8, name=f"{name}_scales", align_bytes=64, offset=offset + 2 * GATHER)
            nc.vector.tensor_copy(out=words[:], in_=xt_word_table[:].indirect(entries))
            nc.vector.tensor_copy(out=scales[:], in_=xt_scale_table[:].indirect(entries))
            return words, scales

        def dealt_matrix(words, scales, groups, name):
            parts = []
            for first, last in groups:
                part_words = deal(words, I32, first, last, f"{name}_words{first}")
                part_scales = deal(scales, U8, first, last, f"{name}_scales{first}")
                for t in range(last - first):
                    cols = slice(t * P, (t + 1) * P)
                    parts.append((part_words[:, cols], part_scales[:, cols]))
            return parts

        def product(acc, matrix_part, tokens, lo, hi):
            nc.tensor.matmul_mx(
                acc, lhsT=matrix_part[0].bitcast(FP8X4), lhsT_scale=matrix_part[1],
                rhs=tokens[0][:, lo:hi].bitcast(FP4X4), rhs_scale=tokens[1][:, lo:hi], start=True, stop=True,
            )

        def slot_results(matrix_part, pieces, on_scalar=False):
            width = sum(hi - lo for tokens, lo, hi in pieces)
            acc = psum_slots.tile([P, width], F32, name="acc")
            at = 0
            for tokens, lo, hi in pieces:
                product(acc[:, at:at + hi - lo], matrix_part, tokens, lo, hi)
                at = at + hi - lo
            result = results.tile([P, width], F32, name="result")
            if on_scalar:
                nc.scalar.activation(out=result[:], in_=acc[:], func=COPY)
            else:
                nc.vector.tensor_copy(out=result[:], in_=acc[:])
            return result

        def scatter(page, entries, values):
            nc.scalar.activation(out=page[:].indirect(entries), in_=values, func=COPY)

        def scatter_on_page(result, lists, t, name):
            page = zeroed(C, f"{name}{t}", AT_PAGES + 4 * C * t)
            scatter(page, lists[:], result[:])
            return page

        def quantise(grouped, width, name):
            codes = keep.tile([P, width], I32, name=f"{name}_codes", align_bytes=64)
            scales = keep.tile([P, width], U8, name=f"{name}_scales", align_bytes=64)
            nc.vector.quantize_mx(out=codes[:].bitcast(FP8X4), scales=scales[:], in_=grouped[:].rearrange("p c t -> p (c t)"))
            return codes, scales

        head_tokens = gather_tokens(0, AT_HEAD, "head")
        w_dealt = dealt_matrix(w_loaded, w_scale_rows, ((0, PACK),), "w")
        first_pages = [zeroed(C, f"first_page{t}", AT_PAGES + 4 * C * t) for t in range(EARLY)]
        early = [slot_results(w_dealt[t], ((head_tokens, 0, GATHER),), on_scalar=True) for t in range(EARLY)]
        for t in range(EARLY):
            scatter(first_pages[t], first_page_lists[:, :GATHER // 16], early[t][:])
        tail_tokens = gather_tokens(J - GATHER, AT_W, "tail")
        for t in range(EARLY):
            result = slot_results(w_dealt[t], ((tail_tokens, 2 * GATHER - J, GATHER),))
            scatter(first_pages[t], first_page_lists[:, GATHER // 16:], result[:])
        all_slots = ((head_tokens, 0, J - GATHER), (tail_tokens, 0, GATHER))

        w2_scale_rows = scale_tile(R, "w2_scale_rows", AT_W_SCALES)
        wb_scale_rows = scale_tile(N, "wb_scale_rows", AT_XT_SCALES)
        wo_scale_rows = scale_tile(N, "wo_scale_rows", AT_XT_SCALES + N)
        w2_loaded = shared.tile([P, R], I32, name="w2_loaded", align_bytes=64, offset=AT_W2)
        load_e4m3_words(w2_loaded, w2_words)
        w2_staged = stage_scale_rows(w2_scales, "w2_staged")
        second_page_lists = load_list(offs3, "second_page_lists")
        wb_loaded = keep.tile([P, N], I32, name="wb_loaded", align_bytes=64)
        load_e4m3_words(wb_loaded, wb_words)
        load_scale_rows(wb_scale_rows, wb_scales)
        wo_loaded = keep.tile([P, 2 * N], U8, name="wo_loaded", align_bytes=64)
        nc.sync.dma_start(wo_loaded[:].bitcast(I32), wo_words[0].bitcast(I32))
        load_scale_rows(wo_scale_rows, wo_scales)
        relay_put_lists = load_list(offs4, "relay_put_lists")
        relay_get_lists = load_list(offs5, "relay_get_lists")
        last_page_lists = load_list(offs6, "last_page_lists")
        relay_weights = []
        for n in range(N // P):
            weight = keep.tile([P, 1], F32, name=f"relay_weight{n}")
            nc.sync.dma_start(weight[:], se[n * P:(n + 1) * P, :])
            relay_weights.append(weight)

        for t in range(EARLY, PACK):
            first_pages.append(scatter_on_page(slot_results(w_dealt[t], all_slots), first_page_lists, t, "first_page"))
        spread_scale_rows(w2_scale_rows, w2_staged)
        w2_dealt = dealt_matrix(w2_loaded, w2_scale_rows, ((0, PACK),), "w2")
        second_results = [slot_results(w2_dealt[t], all_slots) for t in range(PACK)]

        first_grouped = shared.tile([P, C, PACK], BF16, name="first_grouped", align_bytes=64, offset=AT_W2)
        second_pages = []
        for t in range(PACK):
            nc.vector.tensor_copy(out=first_grouped[:, :, t], in_=first_pages[t][:])
            second_pages.append(scatter_on_page(second_results[t], second_page_lists, t, "second_page"))
        first_codes, first_scales = quantise(first_grouped, C, "first")
        relay_pages = [zeroed(U, f"relay_page{n}", offset) for n, offset in enumerate((AT_W, AT_W2))]
        second_grouped = {}
        for run in range(2):
            lo, hi = PAGE_RUNS[run]
            second_grouped[run] = keep.tile([P, hi - lo, PACK], BF16, name=f"second_grouped{run}", tag=f"second_grouped{run}", align_bytes=64)

        def round_second(t, run):
            lo, hi = PAGE_RUNS[run]
            nc.vector.tensor_copy(out=second_grouped[run][:, :, t], in_=second_pages[t][:, lo:hi])

        banks = {}
        for run, (lo, hi) in enumerate(PAGE_RUNS):
            if run == 0:
                for n in range(N // P):
                    single = psum_pages.tile([P, hi - lo], F32, name=f"page_sum{run}_{n}")
                    banks[run, n] = single[:]
            else:
                both = psum_pages.tile([P, N // P, hi - lo], F32, name=f"page_sum{run}")
                banks[run] = both
                for n in range(N // P):
                    banks[run, n] = both[:, n, :]
            for n in range(N // P):
                rows = slice(n * P, (n + 1) * P)
                nc.tensor.matmul_mx(
                    banks[run, n], lhsT=wb_loaded[:, rows].bitcast(FP8X4), lhsT_scale=wb_scale_rows[:, rows],
                    rhs=first_codes[:, lo:hi].bitcast(FP8X4), rhs_scale=first_scales[:, lo:hi],
                    start=(run == 0 or n == 0), stop=False,
                )

        for t in range(PACK - 1):
            for run in range(2):
                round_second(t, run)

        def finish_run(run):
            lo, hi = PAGE_RUNS[run]
            codes, scales = quantise(second_grouped[run], hi - lo, f"second{run}")
            for n in range(N // P):
                nc.tensor.matmul_mx(
                    banks[run, n], lhsT=wo_loaded[:, 2 * n * P:2 * (n + 1) * P].bitcast(FP4X4),
                    lhsT_scale=wo_scale_rows[:, n * P:(n + 1) * P],
                    rhs=codes[:].bitcast(FP8X4), rhs_scale=scales[:],
                    start=False, stop=(run == 0 or n == N // P - 1),
                )

        def relay_run(run):
            lo, hi = PAGE_RUNS[run]
            sums = keep.tile([P, N // P, hi - lo], F32, name=f"sums{run}")
            if run == 0:
                for n in range(N // P):
                    nc.scalar.copy(out=sums[:, n, :], in_=banks[run, n])
            else:
                nc.vector.tensor_copy(out=sums[:], in_=banks[run][:])
            for n in range(N // P):
                scatter(relay_pages[n], relay_put_lists[:, lo // 16:hi // 16], sums[:, n, :])

        round_second(PACK - 1, 0)
        round_second(PACK - 1, 1)
        finish_run(0)
        finish_run(1)
        relay_run(0)
        relay_run(1)
        lo, hi = PAGE_RUNS[2]
        second_grouped[2] = keep.tile([P, hi - lo, PACK], BF16, name="second_grouped2", tag="second_grouped0", align_bytes=64)
        for t in range(PACK):
            round_second(t, 2)
        finish_run(2)
        relay_run(2)
        last_pages = [zeroed(G, f"last_page{n}", AT_PAGES + 4 * C * n) for n in range(N // P)]

        relayed = []
        for n in range(N // P):
            values = keep.tile([P, E], F32, name=f"relayed{n}")
            nc.scalar.activation(
                out=values[:], in_=relay_pages[n][:].indirect(relay_get_lists[:]), func=COPY, scale=relay_weights[n][:]
            )
            relayed.append(values)
        for n in range(N // P):
            nc.scalar.activation(out=last_pages[n][:].indirect(last_page_lists[:]), in_=relayed[n][:], func=COPY)
            nc.sync.dma_start(out[n * P:(n + 1) * P, :], last_pages[n][:])
